import numpy as np
import ml_dtypes


def mxq(x, axis, fmt="e4m3"):
    dtype, down = {"e4m3": (ml_dtypes.float8_e4m3fn, 7), "e5m2": (ml_dtypes.float8_e5m2, 14)}[fmt]
    v = np.moveaxis(np.asarray(x, np.float32).astype(ml_dtypes.bfloat16).astype(np.float64), axis, -1)
    blocks = v.reshape(v.shape[:-1] + (-1, 32))
    amax = np.abs(blocks).max(-1, keepdims=True)
    byte = np.maximum(np.where(amax > 0, np.frexp(amax)[1] - 1 + 127, 0) - down, 1)
    scale = np.exp2(byte - 127.0)
    codes = (blocks / scale).astype(np.float32).astype(dtype).astype(np.float64)
    return np.moveaxis((codes * scale).reshape(v.shape), -1, axis)


WIDE = False


def mx_kscale(k):
    if not WIDE:
        return np.ones(k)
    levels = np.array([10, -10, 5, -5, 0])
    if k % 512:
        return np.exp2(np.random.permutation(np.resize(levels, k // 32))).repeat(32)
    a = np.empty((k // 512, 16))
    for p in range(k // 512):
        a[p, :8] = np.random.permutation(np.resize(levels, 8))
        for g in range(8):
            far = levels[np.abs(levels - a[p, g]) >= 10]
            a[p, g + 8] = far[np.random.randint(len(far))]
    return np.exp2(a.ravel()).repeat(32)


def f64(x):
    return np.asarray(x).astype(np.float64)


def striped(idx):
    return np.tile(idx.reshape(-1, 16).T, (8, 1)).astype(np.uint16)


def unstriped(offs):
    return offs[:16].T.reshape(-1).astype(np.int64)


def striped8(idx):
    return np.concatenate([x.reshape(-1, 16).T for x in idx]).astype(np.uint16)


def runs(offs, k):
    lists = np.stack([offs[16 * r : 16 * r + 16].T.reshape(-1) for r in range(8)]).astype(np.int64)
    return lists[np.arange(k) % 512 // 64]


def pack_weight(w):
    k, n = w.shape
    w = f64(np.asarray(w, np.float32).astype(ml_dtypes.bfloat16)).reshape(k // 32, 32, n)
    amax = np.abs(w).max(1)
    byte = np.clip(np.where(amax > 0, np.frexp(amax)[1] - 1 + 127 - 7, 1), 1, 254)
    scaled = (w * np.exp2(127.0 - byte)[:, None, :]).reshape(k, n).astype(np.float32)
    words = np.ascontiguousarray(scaled.reshape(k // 512, 128, 4, n).transpose(0, 1, 3, 2)).astype(ml_dtypes.float8_e4m3fn).view(np.uint8)
    return words, np.ascontiguousarray(byte.astype(np.uint8).reshape(k // 512, 16, n))


def unpack_weight(words, scales):
    g, p, n, _ = words.shape
    vals = np.ascontiguousarray(words).view(ml_dtypes.float8_e4m3fn).astype(np.float64) * np.repeat(np.exp2(scales.astype(np.float64) - 127.0), 8, axis=1)[..., None]
    return vals.transpose(0, 1, 3, 2).reshape(g * 512, n)


def sigmoid(v):
    return 1.0 / (1.0 + np.exp(-np.maximum(v, -700.0)))

def planes(y):
    n, m = y.shape
    v = y.astype(np.float32).astype(ml_dtypes.bfloat16).astype(np.float64).reshape(n // 32, 32, m)
    top = np.abs(v).max(1)
    byte = np.clip(np.where(top > 0, np.frexp(top)[1] - 1 + 127 - 7, 1), 1, 254)
    codes = (v * np.exp2(127.0 - byte)[:, None, :]).reshape(n, m).astype(np.float32).astype(ml_dtypes.float8_e4m3fn).view(np.uint8)
    words = codes.reshape(n // 512, 128, 4, m).transpose(0, 1, 3, 2)
    return np.ascontiguousarray(words), np.ascontiguousarray(byte.astype(np.uint8).reshape(n // 512, 16, m))


K, T, S, V, N, U, H = 512, 2048, 512, 1024, 512, 1024, 512


def setup_inputs():
    n = np.random.standard_normal
    s = mx_kscale(K)[:, None]
    u = mx_kscale(H)
    packed_xT = pack_weight(n((K, T)) * s)
    packed_w1 = pack_weight(n((K, H)) / np.sqrt(K) / s)
    packed_w2 = pack_weight(n((H, N)) / np.sqrt(H) / u[:, None])
    return {
        "x_words": packed_xT[0],
        "x_scales": packed_xT[1],
        "w1_words": packed_w1[0],
        "w1_scales": packed_w1[1],
        "grid": n((H, U)).astype(np.float32),
        "gn": (np.random.uniform(0.5, 1.5, (H, 1)) * u[:, None]).astype(np.float32),
        "w2_words": packed_w2[0],
        "w2_scales": packed_w2[1],
        "res": (2 * n((N, V))).astype(np.float32),
        "offs": striped(np.random.permutation(T)[:S]),
        "cell": striped8(np.stack([np.random.permutation(U)[:S] for _ in range(8)])),
        "look": striped8(np.stack([np.random.permutation(U) for _ in range(8)])),
    }


def reference(x_words, x_scales, w1_words, w1_scales, grid, gn, w2_words, w2_scales, res, offs, cell, look):
    xq = unpack_weight(x_words, x_scales)[:, unstriped(offs)]
    p = np.clip(sigmoid(unpack_weight(w1_words, w1_scales).T @ xq), 0.1, 0.9)
    nw = np.clip(f64(grid)[np.arange(H)[:, None], runs(cell, H)] + np.log(p / (-1.0 * p + 1)), -2.0, 2.0)
    gd = f64(grid).copy()
    gd[np.arange(H)[:, None], runs(cell, H)] = nw
    z = f64(gn) * (gd[np.arange(H)[:, None], runs(look, H)])
    out_0 = f64(res) + (unpack_weight(w2_words, w2_scales).T @ mxq(z, 0, "e4m3"))
    return (out_0,) + planes(out_0)

@@ -1,0 +1,207 @@
+import math
+from contextlib import ExitStack
+
+import concourse.mybir as mybir
+
+K, T, S, V, N, U, H = 512, 2048, 512, 1024, 512, 1024, 512
+FLOPS = 2 * K * H * S + 2 * H * N * V
+
+F32 = mybir.dt.float32
+BF16 = mybir.dt.bfloat16
+I32 = mybir.dt.int32
+U32 = mybir.dt.uint32
+U16 = mybir.dt.uint16
+U8 = mybir.dt.uint8
+FP8X4 = mybir.dt.float8_e4m3fn_x4
+ALU = mybir.AluOpType
+COPY = mybir.ActivationFunctionType.Copy
+RELU = mybir.ActivationFunctionType.Relu
+
+P = 128
+PACK = 4
+QUADS = 4
+CHUNK = 256
+PIECE = 128
+LOGIT_BOUND = math.log(0.9 / 0.1)
+ODDS_BOUND = 2.0
+
+
+def load_scale_rows(queue, plane, rows):
+    for q in range(QUADS):
+        queue.dma_start(out=plane[32 * q : 32 * q + 4, :].bitcast(I32), in_=rows[0, 4 * q : 4 * q + 4, :].bitcast(I32))
+
+
+def packed_words(words):
+    return words[0].rearrange("p n t -> p (n t)").bitcast(I32)
+
+
+def tile_picked_occread_none_po_kernel(
+    tc, x_words, x_scales, w1_words, w1_scales, grid, gn, w2_words, w2_scales, res, offs, cell, look, out_0, out_1, out_2
+):
+    nc = tc.nc
+    chunks = V // CHUNK
+    with ExitStack() as ctx:
+        keep = ctx.enter_context(tc.tile_pool(name="keep", bufs=1))
+        ring = ctx.enter_context(tc.tile_pool(name="ring", bufs=2))
+        deep = ctx.enter_context(tc.tile_pool(name="deep", bufs=4))
+        psum = ctx.enter_context(tc.psum_pool(name="psum", bufs=1))
+
+        offs_t = keep.tile([P, S // 16], U16, name="offs_t")
+        cell_t = keep.tile([P, S // 16], U16, name="cell_t")
+        look_t = keep.tile([P, V // 16], U16, name="look_t")
+        x_w = keep.tile([P, T], I32, name="x_w", align_bytes=64)
+        x_s = keep.tile([P, T], U8, name="x_s", align_bytes=64)
+        w1_w = keep.tile([P, H], I32, name="w1_w", align_bytes=64)
+        w1_s = keep.tile([P, H], U8, name="w1_s", align_bytes=64)
+        w2_w = keep.tile([P, N], I32, name="w2_w", align_bytes=64)
+        w2_s = keep.tile([P, N], U8, name="w2_s", align_bytes=64)
+        gn_t = keep.tile([P, PACK], F32, name="gn_t")
+        gd = [keep.tile([P, U], F32, name="gd%d" % t, align_bytes=64) for t in range(PACK)]
+        res_t = [keep.tile([P, PACK, V // 2], F32, name="res%d" % h, align_bytes=64) for h in range(2)]
+
+        nc.gpsimd.memset(w1_s[:].bitcast(I32), 0)
+        nc.vector.memset(x_s[:].bitcast(I32), 0)
+        nc.vector.memset(w2_s[:].bitcast(I32), 0)
+
+        grid_rows = grid.rearrange("(p t) u -> p t u", t=PACK)
+        res_rows = res.rearrange("(p t) v -> p t v", t=PACK)
+        out_rows = out_0.rearrange("(p t) v -> p t v", t=PACK)
+        nc.sync.dma_start(offs_t[:], offs)
+        nc.sync.dma_start(cell_t[:], cell)
+        nc.sync.dma_start(out=w1_w[:], in_=packed_words(w1_words))
+        load_scale_rows(nc.sync, w1_s, w1_scales)
+        nc.sync.dma_start(out=x_w[:], in_=packed_words(x_words))
+        load_scale_rows(nc.sync, x_s, x_scales)
+        for t in range(PACK):
+            nc.sync.dma_start(out=gd[t][:], in_=grid_rows[:, t, :])
+        nc.sync.dma_start(out=w2_w[:], in_=packed_words(w2_words))
+        load_scale_rows(nc.sync, w2_s, w2_scales)
+        nc.sync.dma_start(out=gn_t[:], in_=gn.rearrange("(p t) o -> p (t o)", t=PACK))
+        nc.sync.dma_start(look_t[:], look)
+        for h in range(2):
+            nc.sync.dma_start(out=res_t[h][:], in_=res_rows[:, :, h * (V // 2) : (h + 1) * (V // 2)])
+
+        def deal(words, plane, tag_w, tag_s):
+            dealt_w = keep.tile([P, PACK, P], I32, name="dealt_w", tag=tag_w, align_bytes=64)
+            dealt_s = keep.tile([P, PACK, P], U8, name="dealt_s", tag=tag_s, align_bytes=64)
+            nc.vector.tensor_copy(out=dealt_w[:], in_=words[:].rearrange("p (m t) -> p t m", t=PACK))
+            nc.vector.tensor_copy(out=dealt_s[:], in_=plane[:].rearrange("p (m t) -> p t m", t=PACK))
+            return dealt_w, dealt_s
+
+        half = S // 2
+        minus_bound = keep.tile([P, S], F32, name="minus_bound", align_bytes=64)
+        nc.vector.memset(minus_bound[:], -ODDS_BOUND)
+        sums = [keep.tile([P, S], F32, name="moved%d" % t, align_bytes=64) for t in range(PACK)]
+        w1_dw, w1_ds = deal(w1_w, w1_s, "w1_dw", "w1_ds")
+        banks = {}
+        for h in range(2):
+            xg_w = keep.tile([P, half], U32, name="xg_w%d" % h, align_bytes=64)
+            xg_s = keep.tile([P, half], U8, name="xg_s%d" % h, align_bytes=64)
+            picks = offs_t[:, h * half // 16 : (h + 1) * half // 16]
+            nc.vector.tensor_copy(out=xg_w[:], in_=x_w[:].bitcast(U32).indirect(picks))
+            nc.vector.tensor_copy(out=xg_s[:], in_=x_s[:].indirect(picks))
+            for u in range(2):
+                bank = psum.tile([P, 2, half], F32, name="logit%d" % (2 * h + u))
+                for e in range(2):
+                    t = 2 * u + e
+                    nc.tensor.matmul_mx(
+                        out=bank[:, e, :], lhsT=w1_dw[:, t, :].bitcast(FP8X4), lhsT_scale=w1_ds[:, t, :],
+                        rhs=xg_w[:].bitcast(FP8X4), rhs_scale=xg_s[:], start=True, stop=True,
+                    )
+                banks[h, u] = bank
+        for u in range(2):
+            for h in range(2):
+                below = ring.tile([P, 2, half], F32, name="below", align_bytes=64)
+                nc.scalar.activation(below[:], banks[h, u][:], RELU, bias=LOGIT_BOUND, scale=-1.0)
+                step = keep.tile([P, 2, half], F32, name="step", tag="step%d" % (2 * u + h), align_bytes=64)
+                nc.scalar.activation(step[:], below[:], RELU, bias=2 * LOGIT_BOUND, scale=-1.0)
+                hits = cell_t[:, h * half // 16 : (h + 1) * half // 16]
+                for e in range(2):
+                    t = 2 * u + e
+                    nc.vector.tensor_tensor(sums[t][:, h * half : (h + 1) * half], gd[t][:].indirect(hits), step[:, e, :], ALU.add)
+        w2_dw, w2_ds = deal(w2_w, w2_s, "step2", "step3")
+
+        lifted, gained = {}, []
+
+        def clip(t):
+            room = ring.tile([P, S], F32, name="room", align_bytes=64)
+            nc.scalar.activation(room[:], sums[t][:], RELU, bias=LOGIT_BOUND + ODDS_BOUND, scale=-1.0)
+            nw = ring.tile([P, S], F32, name="nw", tag="stage", align_bytes=64)
+            nc.scalar.activation(nw[:], room[:], RELU, bias=2 * ODDS_BOUND, scale=-1.0)
+            lifted[t] = nw
+
+        def put_back(t):
+            nc.vector.tensor_tensor(gd[t][:].indirect(cell_t[:]), lifted[t][:], minus_bound[:], ALU.add)
+            zf = keep.tile([P, U], F32, name="gained%d" % t, align_bytes=64)
+            nc.scalar.activation(zf[:], gd[t][:], COPY, scale=gn_t[:, t : t + 1])
+            gained.append(zf)
+
+        for t in range(PACK + 1):
+            if t < PACK:
+                clip(t)
+            if t > 0:
+                put_back(t - 1)
+
+        y_w = keep.tile([P, V], I32, name="y_w", align_bytes=64)
+        y_s = keep.tile([P, V], U8, name="y_s", align_bytes=64)
+        y = [keep.tile([P, PACK, CHUNK], F32, name="y%d" % c, align_bytes=64) for c in range(chunks)]
+        out_words = packed_words(out_1)
+        state = {}
+        per = CHUNK // PIECE
+        pieces = V // PIECE
+
+        def fetch(c):
+            planes = ring.tile([P, PACK, CHUNK], BF16, name="planes", tag="stage", align_bytes=64)
+            entries = look_t[:, c * CHUNK // 16 : (c + 1) * CHUNK // 16]
+            for t in range(PACK):
+                nc.vector.tensor_copy(out=planes[:, t, :], in_=gained[t][:].indirect(entries))
+            for j in range(per):
+                woven = deep.tile([P, PIECE, PACK], BF16, name="woven", align_bytes=64)
+                nc.scalar.copy(out=woven[:], in_=planes[:, :, j * PIECE : (j + 1) * PIECE].rearrange("p t n -> p n t"))
+                state["woven", c * per + j] = woven
+
+        def multiply(i):
+            z_w = deep.tile([P, PIECE], U32, name="z_w", align_bytes=64)
+            z_s = deep.tile([P, PIECE], U8, name="z_s", align_bytes=64)
+            nc.vector.quantize_mx(out=z_w[:].bitcast(FP8X4), scales=z_s[:], in_=state["woven", i][:].rearrange("p n t -> p (n t)"))
+            bank = psum.tile([P, PACK, PIECE], F32, name="prod%d" % (i % 4))
+            for t in range(PACK):
+                nc.tensor.matmul_mx(
+                    out=bank[:, t, :], lhsT=w2_dw[:, t, :].bitcast(FP8X4), lhsT_scale=w2_ds[:, t, :],
+                    rhs=z_w[:].bitcast(FP8X4), rhs_scale=z_s[:], start=True, stop=True,
+                )
+            state["bank", i] = bank
+
+        def finish(i):
+            c, j = divmod(i, per)
+            part = y[c][:, :, j * PIECE : (j + 1) * PIECE]
+            h, first = divmod(i * PIECE, V // 2)
+            nc.vector.tensor_tensor(part, state["bank", i][:], res_t[h][:, :, first : first + PIECE], ALU.add)
+            if c == chunks - 1:
+                nc.sync.dma_start(out=out_rows[:, :, i * PIECE : (i + 1) * PIECE], in_=part)
+            elif j == per - 1:
+                nc.sync.dma_start(out=out_rows[:, :, c * CHUNK : (c + 1) * CHUNK], in_=y[c][:])
+            rounded = deep.tile([P, PIECE, PACK], BF16, name="rounded", align_bytes=64)
+            nc.scalar.copy(out=rounded[:], in_=part.rearrange("p t n -> p n t"))
+            state["rounded", i] = rounded
+
+        def hand_on(i):
+            cols = slice(i * PIECE, (i + 1) * PIECE)
+            nc.vector.quantize_mx(out=y_w[:, cols].bitcast(FP8X4), scales=y_s[:, cols], in_=state["rounded", i][:].rearrange("p n t -> p (n t)"))
+            if i % per == per - 1:
+                done = slice((i + 1 - per) * PIECE, (i + 1) * PIECE)
+                nc.sync.dma_start(out=out_words[:, done], in_=y_w[:, done])
+
+        fetch(0)
+        fetch(1)
+        for i in range(pieces + 3):
+            if i < pieces:
+                multiply(i)
+            if i % per == per - 1 and i // per + 2 < chunks:
+                fetch(i // per + 2)
+            if 0 <= i - 3 < pieces:
+                hand_on(i - 3)
+            if 0 <= i - 1 < pieces:
+                finish(i - 1)
+        for q in range(QUADS):
+            nc.sync.dma_start(out=out_2[0, 4 * q : 4 * q + 4, :].bitcast(I32), in_=y_s[32 * q : 32 * q + 4, :].bitcast(I32))

@@ -22,6 +22,7 @@ PACK = 4
 QUADS = 4
 CHUNK = 256
 PIECE = 128
+RUN = 4
 LOGIT_BOUND = math.log(0.9 / 0.1)
 ODDS_BOUND = 2.0
 
@@ -66,12 +67,12 @@ def tile_picked_occread_none_po_kernel(
         grid_rows = grid.rearrange("(p t) u -> p t u", t=PACK)
         res_rows = res.rearrange("(p t) v -> p t v", t=PACK)
         out_rows = out_0.rearrange("(p t) v -> p t v", t=PACK)
-        nc.sync.dma_start(offs_t[:], offs)
-        nc.sync.dma_start(cell_t[:], cell)
         nc.sync.dma_start(out=w1_w[:], in_=packed_words(w1_words))
         load_scale_rows(nc.sync, w1_s, w1_scales)
         nc.sync.dma_start(out=x_w[:], in_=packed_words(x_words))
+        nc.sync.dma_start(offs_t[:], offs)
         load_scale_rows(nc.sync, x_s, x_scales)
+        nc.sync.dma_start(cell_t[:], cell)
         for t in range(PACK):
             nc.sync.dma_start(out=gd[t][:], in_=grid_rows[:, t, :])
         nc.sync.dma_start(out=w2_w[:], in_=packed_words(w2_words))
@@ -100,26 +101,23 @@ def tile_picked_occread_none_po_kernel(
             picks = offs_t[:, h * half // 16 : (h + 1) * half // 16]
             nc.vector.tensor_copy(out=xg_w[:], in_=x_w[:].bitcast(U32).indirect(picks))
             nc.vector.tensor_copy(out=xg_s[:], in_=x_s[:].indirect(picks))
-            for u in range(2):
-                bank = psum.tile([P, 2, half], F32, name="logit%d" % (2 * h + u))
-                for e in range(2):
-                    t = 2 * u + e
-                    nc.tensor.matmul_mx(
-                        out=bank[:, e, :], lhsT=w1_dw[:, t, :].bitcast(FP8X4), lhsT_scale=w1_ds[:, t, :],
-                        rhs=xg_w[:].bitcast(FP8X4), rhs_scale=xg_s[:], start=True, stop=True,
-                    )
-                banks[h, u] = bank
+            for t in range(PACK):
+                bank = psum.tile([P, half], F32, name="logit", tag="bank%d" % (PACK * h + t))
+                nc.tensor.matmul_mx(
+                    out=bank[:], lhsT=w1_dw[:, t, :].bitcast(FP8X4), lhsT_scale=w1_ds[:, t, :],
+                    rhs=xg_w[:].bitcast(FP8X4), rhs_scale=xg_s[:], start=True, stop=True,
+                )
+                banks[h, t] = bank
         for u in range(2):
             for h in range(2):
-                below = ring.tile([P, 2, half], F32, name="below", align_bytes=64)
-                nc.scalar.activation(below[:], banks[h, u][:], RELU, bias=LOGIT_BOUND, scale=-1.0)
-                step = keep.tile([P, 2, half], F32, name="step", tag="step%d" % (2 * u + h), align_bytes=64)
-                nc.scalar.activation(step[:], below[:], RELU, bias=2 * LOGIT_BOUND, scale=-1.0)
                 hits = cell_t[:, h * half // 16 : (h + 1) * half // 16]
-                for e in range(2):
-                    t = 2 * u + e
-                    nc.vector.tensor_tensor(sums[t][:, h * half : (h + 1) * half], gd[t][:].indirect(hits), step[:, e, :], ALU.add)
-        w2_dw, w2_ds = deal(w2_w, w2_s, "step2", "step3")
+                for t in (2 * u, 2 * u + 1):
+                    below = ring.tile([P, half], F32, name="below", align_bytes=64)
+                    nc.scalar.activation(below[:], banks[h, t][:], RELU, bias=LOGIT_BOUND, scale=-1.0)
+                    step = keep.tile([P, half], F32, name="step", tag="step%d" % (PACK * h + t), align_bytes=64)
+                    nc.scalar.activation(step[:], below[:], RELU, bias=2 * LOGIT_BOUND, scale=-1.0)
+                    nc.vector.tensor_tensor(sums[t][:, h * half : (h + 1) * half], gd[t][:].indirect(hits), step[:], ALU.add)
+        w2_dw, w2_ds = deal(w2_w, w2_s, "step6", "step7")
 
         lifted, gained = {}, []
 
@@ -157,14 +155,17 @@ def tile_picked_occread_none_po_kernel(
                 nc.vector.tensor_copy(out=planes[:, t, :], in_=gained[t][:].indirect(entries))
             for j in range(per):
                 woven = deep.tile([P, PIECE, PACK], BF16, name="woven", align_bytes=64)
-                nc.scalar.copy(out=woven[:], in_=planes[:, :, j * PIECE : (j + 1) * PIECE].rearrange("p t n -> p n t"))
+                nc.scalar.copy(
+                    out=woven[:].rearrange("p (c i) t -> p c t i", i=RUN),
+                    in_=planes[:, :, j * PIECE : (j + 1) * PIECE].rearrange("p t (c i) -> p c t i", i=RUN),
+                )
                 state["woven", c * per + j] = woven
 
         def multiply(i):
             z_w = deep.tile([P, PIECE], U32, name="z_w", align_bytes=64)
             z_s = deep.tile([P, PIECE], U8, name="z_s", align_bytes=64)
             nc.vector.quantize_mx(out=z_w[:].bitcast(FP8X4), scales=z_s[:], in_=state["woven", i][:].rearrange("p n t -> p (n t)"))
-            bank = psum.tile([P, PACK, PIECE], F32, name="prod%d" % (i % 4))
+            bank = psum.tile([P, PACK, PIECE], F32, name="prod", tag="bank%d" % i)
             for t in range(PACK):
                 nc.tensor.matmul_mx(
                     out=bank[:, t, :], lhsT=w2_dw[:, t, :].bitcast(FP8X4), lhsT_scale=w2_ds[:, t, :],
@@ -182,7 +183,9 @@ def tile_picked_occread_none_po_kernel(
             elif j == per - 1:
                 nc.sync.dma_start(out=out_rows[:, :, c * CHUNK : (c + 1) * CHUNK], in_=y[c][:])
             rounded = deep.tile([P, PIECE, PACK], BF16, name="rounded", align_bytes=64)
-            nc.scalar.copy(out=rounded[:], in_=part.rearrange("p t n -> p n t"))
+            nc.scalar.copy(
+                out=rounded[:].rearrange("p (c i) t -> p c t i", i=RUN), in_=part.rearrange("p t (c i) -> p c t i", i=RUN)
+            )
             state["rounded", i] = rounded
 
         def hand_on(i):

@@ -44,7 +44,6 @@ def tile_picked_occread_none_po_kernel(
     with ExitStack() as ctx:
         keep = ctx.enter_context(tc.tile_pool(name="keep", bufs=1))
         ring = ctx.enter_context(tc.tile_pool(name="ring", bufs=2))
-        deep = ctx.enter_context(tc.tile_pool(name="deep", bufs=4))
         psum = ctx.enter_context(tc.psum_pool(name="psum", bufs=1))
 
         offs_t = keep.tile([P, S // 16], U16, name="offs_t")
@@ -57,7 +56,7 @@ def tile_picked_occread_none_po_kernel(
         w2_w = keep.tile([P, N], I32, name="w2_w", align_bytes=64)
         w2_s = keep.tile([P, N], U8, name="w2_s", align_bytes=64)
         gn_t = keep.tile([P, PACK], F32, name="gn_t")
-        gd = [keep.tile([P, U], F32, name="gd%d" % t, align_bytes=64) for t in range(PACK)]
+        gd = [keep.tile([P, U], F32, name="gd", tag="gd%d" % t, align_bytes=64) for t in range(PACK)]
         res_t = [keep.tile([P, PACK, V // 2], F32, name="res%d" % h, align_bytes=64) for h in range(2)]
 
         nc.gpsimd.memset(w1_s[:].bitcast(I32), 0)
@@ -85,8 +84,11 @@ def tile_picked_occread_none_po_kernel(
         def deal(words, plane, tag_w, tag_s):
             dealt_w = keep.tile([P, PACK, P], I32, name="dealt_w", tag=tag_w, align_bytes=64)
             dealt_s = keep.tile([P, PACK, P], U8, name="dealt_s", tag=tag_s, align_bytes=64)
-            nc.vector.tensor_copy(out=dealt_w[:], in_=words[:].rearrange("p (m t) -> p t m", t=PACK))
-            nc.vector.tensor_copy(out=dealt_s[:], in_=plane[:].rearrange("p (m t) -> p t m", t=PACK))
+            for dealt, packed in ((dealt_w, words), (dealt_s, plane)):
+                nc.vector.tensor_copy(
+                    out=dealt[:].rearrange("p t (c i) -> p c t i", i=RUN),
+                    in_=packed[:].rearrange("p (c i t) -> p c t i", i=RUN, t=PACK),
+                )
             return dealt_w, dealt_s
 
         half = S // 2
@@ -144,67 +146,55 @@ def tile_picked_occread_none_po_kernel(
         y_s = keep.tile([P, V], U8, name="y_s", align_bytes=64)
         y = [keep.tile([P, PACK, CHUNK], F32, name="y%d" % c, align_bytes=64) for c in range(chunks)]
         out_words = packed_words(out_1)
-        state = {}
-        per = CHUNK // PIECE
-        pieces = V // PIECE
+        woven = [keep.tile([P, CHUNK, PACK], BF16, name="woven%d" % c, align_bytes=64) for c in range(chunks)]
+        rounded = [keep.tile([P, CHUNK, PACK], BF16, name="rounded%d" % c, align_bytes=64) for c in range(chunks)]
+        z_w = keep.tile([P, V], U32, name="z_w", align_bytes=64)
+        z_s = keep.tile([P, V], U8, name="z_s", align_bytes=64)
 
-        def fetch(c):
-            planes = ring.tile([P, PACK, CHUNK], BF16, name="planes", tag="stage", align_bytes=64)
+        def weave(pairs, rows):
+            nc.scalar.copy(out=pairs.rearrange("p (c i) t -> p c t i", i=RUN), in_=rows.rearrange("p t (c i) -> p c t i", i=RUN))
+
+        for c in range(chunks):
+            if c == 2:
+                planes = keep.tile([P, PACK, CHUNK], BF16, name="planes", tag="gd3", align_bytes=64)
+            else:
+                planes = ring.tile([P, PACK, CHUNK], BF16, name="planes", tag="stage", align_bytes=64)
             entries = look_t[:, c * CHUNK // 16 : (c + 1) * CHUNK // 16]
             for t in range(PACK):
                 nc.vector.tensor_copy(out=planes[:, t, :], in_=gained[t][:].indirect(entries))
-            for j in range(per):
-                woven = deep.tile([P, PIECE, PACK], BF16, name="woven", align_bytes=64)
-                nc.scalar.copy(
-                    out=woven[:].rearrange("p (c i) t -> p c t i", i=RUN),
-                    in_=planes[:, :, j * PIECE : (j + 1) * PIECE].rearrange("p t (c i) -> p c t i", i=RUN),
-                )
-                state["woven", c * per + j] = woven
+            for inner in range(0, CHUNK, PIECE):
+                weave(woven[c][:, inner : inner + PIECE, :], planes[:, :, inner : inner + PIECE])
 
-        def multiply(i):
-            z_w = deep.tile([P, PIECE], U32, name="z_w", align_bytes=64)
-            z_s = deep.tile([P, PIECE], U8, name="z_s", align_bytes=64)
-            nc.vector.quantize_mx(out=z_w[:].bitcast(FP8X4), scales=z_s[:], in_=state["woven", i][:].rearrange("p n t -> p (n t)"))
-            bank = psum.tile([P, PACK, PIECE], F32, name="prod", tag="bank%d" % i)
+        prods = []
+        for first in range(0, V, PIECE):
+            c, inner = divmod(first, CHUNK)
+            cols = slice(first, first + PIECE)
+            nc.vector.quantize_mx(
+                out=z_w[:, cols].bitcast(FP8X4), scales=z_s[:, cols],
+                in_=woven[c][:, inner : inner + PIECE, :].rearrange("p n t -> p (n t)"),
+            )
+            bank = psum.tile([P, PACK, PIECE], F32, name="prod", tag="bank%d" % (first // PIECE))
             for t in range(PACK):
                 nc.tensor.matmul_mx(
                     out=bank[:, t, :], lhsT=w2_dw[:, t, :].bitcast(FP8X4), lhsT_scale=w2_ds[:, t, :],
-                    rhs=z_w[:].bitcast(FP8X4), rhs_scale=z_s[:], start=True, stop=True,
+                    rhs=z_w[:, cols].bitcast(FP8X4), rhs_scale=z_s[:, cols], start=True, stop=True,
                 )
-            state["bank", i] = bank
+            prods.append(bank)
 
-        def finish(i):
-            c, j = divmod(i, per)
-            part = y[c][:, :, j * PIECE : (j + 1) * PIECE]
-            h, first = divmod(i * PIECE, V // 2)
-            nc.vector.tensor_tensor(part, state["bank", i][:], res_t[h][:, :, first : first + PIECE], ALU.add)
-            if c == chunks - 1:
-                nc.sync.dma_start(out=out_rows[:, :, i * PIECE : (i + 1) * PIECE], in_=part)
-            elif j == per - 1:
+        for first in range(0, V, PIECE):
+            c, inner = divmod(first, CHUNK)
+            h, place = divmod(first, V // 2)
+            part = y[c][:, :, inner : inner + PIECE]
+            nc.vector.tensor_tensor(part, prods[first // PIECE][:], res_t[h][:, :, place : place + PIECE], ALU.add)
+            weave(rounded[c][:, inner : inner + PIECE, :], part)
+            if inner + PIECE == CHUNK:
                 nc.sync.dma_start(out=out_rows[:, :, c * CHUNK : (c + 1) * CHUNK], in_=y[c][:])
-            rounded = deep.tile([P, PIECE, PACK], BF16, name="rounded", align_bytes=64)
-            nc.scalar.copy(
-                out=rounded[:].rearrange("p (c i) t -> p c t i", i=RUN), in_=part.rearrange("p t (c i) -> p c t i", i=RUN)
-            )
-            state["rounded", i] = rounded
 
-        def hand_on(i):
-            cols = slice(i * PIECE, (i + 1) * PIECE)
-            nc.vector.quantize_mx(out=y_w[:, cols].bitcast(FP8X4), scales=y_s[:, cols], in_=state["rounded", i][:].rearrange("p n t -> p (n t)"))
-            if i % per == per - 1:
-                done = slice((i + 1 - per) * PIECE, (i + 1) * PIECE)
-                nc.sync.dma_start(out=out_words[:, done], in_=y_w[:, done])
-
-        fetch(0)
-        fetch(1)
-        for i in range(pieces + 3):
-            if i < pieces:
-                multiply(i)
-            if i % per == per - 1 and i // per + 2 < chunks:
-                fetch(i // per + 2)
-            if 0 <= i - 3 < pieces:
-                hand_on(i - 3)
-            if 0 <= i - 1 < pieces:
-                finish(i - 1)
+        for c in range(chunks):
+            cols = slice(c * CHUNK, (c + 1) * CHUNK)
+            nc.vector.quantize_mx(out=y_w[:, cols].bitcast(FP8X4), scales=y_s[:, cols], in_=rounded[c][:].rearrange("p n t -> p (n t)"))
+        for cols in (slice(0, V - CHUNK), slice(V - CHUNK, V)):
+            nc.sync.dma_start(out=out_words[:, cols], in_=y_w[:, cols])
         for q in range(QUADS):
-            nc.sync.dma_start(out=out_2[0, 4 * q : 4 * q + 4, :].bitcast(I32), in_=y_s[32 * q : 32 * q + 4, :].bitcast(I32))
+            queue = nc.scalar if q % 2 else nc.sync
+            queue.dma_start(out=out_2[0, 4 * q : 4 * q + 4, :].bitcast(I32), in_=y_s[32 * q : 32 * q + 4, :].bitcast(I32))

import math
from contextlib import ExitStack

import concourse.mybir as mybir

K, T, S, V, N, U, H = 512, 2048, 512, 1024, 512, 1024, 512
FLOPS = 2 * K * H * S + 2 * H * N * V

F32 = mybir.dt.float32
BF16 = mybir.dt.bfloat16
I32 = mybir.dt.int32
U32 = mybir.dt.uint32
U16 = mybir.dt.uint16
U8 = mybir.dt.uint8
FP8X4 = mybir.dt.float8_e4m3fn_x4
ALU = mybir.AluOpType
COPY = mybir.ActivationFunctionType.Copy
RELU = mybir.ActivationFunctionType.Relu

P = 128
PACK = 4
QUADS = 4
CHUNK = 256
PIECE = 128
RUN = 4
LOGIT_BOUND = math.log(0.9 / 0.1)
ODDS_BOUND = 2.0


def load_scale_rows(queue, plane, rows):
    for q in range(QUADS):
        queue.dma_start(out=plane[32 * q : 32 * q + 4, :].bitcast(I32), in_=rows[0, 4 * q : 4 * q + 4, :].bitcast(I32))


def packed_words(words):
    return words[0].rearrange("p n t -> p (n t)").bitcast(I32)


def tile_picked_occread_none_po_kernel(
    tc, x_words, x_scales, w1_words, w1_scales, grid, gn, w2_words, w2_scales, res, offs, cell, look, out_0, out_1, out_2
):
    nc = tc.nc
    chunks = V // CHUNK
    with ExitStack() as ctx:
        keep = ctx.enter_context(tc.tile_pool(name="keep", bufs=1))
        ring = ctx.enter_context(tc.tile_pool(name="ring", bufs=2))
        psum = ctx.enter_context(tc.psum_pool(name="psum", bufs=1))

        offs_t = keep.tile([P, S // 16], U16, name="offs_t")
        cell_t = keep.tile([P, S // 16], U16, name="cell_t")
        look_t = keep.tile([P, V // 16], U16, name="look_t")
        x_w = keep.tile([P, T], I32, name="x_w", align_bytes=64)
        x_s = keep.tile([P, T], U8, name="x_s", align_bytes=64)
        w1_w = keep.tile([P, H], I32, name="w1_w", align_bytes=64)
        w1_s = keep.tile([P, H], U8, name="w1_s", align_bytes=64)
        w2_w = keep.tile([P, N], I32, name="w2_w", align_bytes=64)
        w2_s = keep.tile([P, N], U8, name="w2_s", align_bytes=64)
        gn_t = keep.tile([P, PACK], F32, name="gn_t")
        gd = [keep.tile([P, U], F32, name="gd", tag="gd%d" % t, align_bytes=64) for t in range(PACK)]
        res_t = [keep.tile([P, PACK, V // 2], F32, name="res%d" % h, align_bytes=64) for h in range(2)]

        nc.gpsimd.memset(w1_s[:].bitcast(I32), 0)
        nc.vector.memset(x_s[:].bitcast(I32), 0)
        nc.vector.memset(w2_s[:].bitcast(I32), 0)

        grid_rows = grid.rearrange("(p t) u -> p t u", t=PACK)
        res_rows = res.rearrange("(p t) v -> p t v", t=PACK)
        out_rows = out_0.rearrange("(p t) v -> p t v", t=PACK)
        nc.sync.dma_start(out=w1_w[:], in_=packed_words(w1_words))
        load_scale_rows(nc.sync, w1_s, w1_scales)
        nc.sync.dma_start(out=x_w[:], in_=packed_words(x_words))
        nc.sync.dma_start(offs_t[:], offs)
        load_scale_rows(nc.sync, x_s, x_scales)
        nc.sync.dma_start(cell_t[:], cell)
        for t in range(PACK):
            nc.sync.dma_start(out=gd[t][:], in_=grid_rows[:, t, :])
        nc.sync.dma_start(out=w2_w[:], in_=packed_words(w2_words))
        load_scale_rows(nc.sync, w2_s, w2_scales)
        nc.sync.dma_start(out=gn_t[:], in_=gn.rearrange("(p t) o -> p (t o)", t=PACK))
        nc.sync.dma_start(look_t[:], look)
        for h in range(2):
            nc.sync.dma_start(out=res_t[h][:], in_=res_rows[:, :, h * (V // 2) : (h + 1) * (V // 2)])

        def deal(words, plane, tag_w, tag_s):
            dealt_w = keep.tile([P, PACK, P], I32, name="dealt_w", tag=tag_w, align_bytes=64)
            dealt_s = keep.tile([P, PACK, P], U8, name="dealt_s", tag=tag_s, align_bytes=64)
            for dealt, packed in ((dealt_w, words), (dealt_s, plane)):
                nc.vector.tensor_copy(
                    out=dealt[:].rearrange("p t (c i) -> p c t i", i=RUN),
                    in_=packed[:].rearrange("p (c i t) -> p c t i", i=RUN, t=PACK),
                )
            return dealt_w, dealt_s

        half = S // 2
        minus_bound = keep.tile([P, S], F32, name="minus_bound", align_bytes=64)
        nc.vector.memset(minus_bound[:], -ODDS_BOUND)
        sums = [keep.tile([P, S], F32, name="moved%d" % t, align_bytes=64) for t in range(PACK)]
        w1_dw, w1_ds = deal(w1_w, w1_s, "w1_dw", "w1_ds")
        banks = {}
        for h in range(2):
            xg_w = keep.tile([P, half], U32, name="xg_w%d" % h, align_bytes=64)
            xg_s = keep.tile([P, half], U8, name="xg_s%d" % h, align_bytes=64)
            picks = offs_t[:, h * half // 16 : (h + 1) * half // 16]
            nc.vector.tensor_copy(out=xg_w[:], in_=x_w[:].bitcast(U32).indirect(picks))
            nc.vector.tensor_copy(out=xg_s[:], in_=x_s[:].indirect(picks))
            for t in range(PACK):
                bank = psum.tile([P, half], F32, name="logit", tag="bank%d" % (PACK * h + t))
                nc.tensor.matmul_mx(
                    out=bank[:], lhsT=w1_dw[:, t, :].bitcast(FP8X4), lhsT_scale=w1_ds[:, t, :],
                    rhs=xg_w[:].bitcast(FP8X4), rhs_scale=xg_s[:], start=True, stop=True,
                )
                banks[h, t] = bank
        for u in range(2):
            for h in range(2):
                hits = cell_t[:, h * half // 16 : (h + 1) * half // 16]
                for t in (2 * u, 2 * u + 1):
                    below = ring.tile([P, half], F32, name="below", align_bytes=64)
                    nc.scalar.activation(below[:], banks[h, t][:], RELU, bias=LOGIT_BOUND, scale=-1.0)
                    step = keep.tile([P, half], F32, name="step", tag="step%d" % (PACK * h + t), align_bytes=64)
                    nc.scalar.activation(step[:], below[:], RELU, bias=2 * LOGIT_BOUND, scale=-1.0)
                    nc.vector.tensor_tensor(sums[t][:, h * half : (h + 1) * half], gd[t][:].indirect(hits), step[:], ALU.add)
        w2_dw, w2_ds = deal(w2_w, w2_s, "step6", "step7")

        lifted, gained = {}, []

        def clip(t):
            room = ring.tile([P, S], F32, name="room", align_bytes=64)
            nc.scalar.activation(room[:], sums[t][:], RELU, bias=LOGIT_BOUND + ODDS_BOUND, scale=-1.0)
            nw = ring.tile([P, S], F32, name="nw", tag="stage", align_bytes=64)
            nc.scalar.activation(nw[:], room[:], RELU, bias=2 * ODDS_BOUND, scale=-1.0)
            lifted[t] = nw

        def put_back(t):
            nc.vector.tensor_tensor(gd[t][:].indirect(cell_t[:]), lifted[t][:], minus_bound[:], ALU.add)
            zf = keep.tile([P, U], F32, name="gained%d" % t, align_bytes=64)
            nc.scalar.activation(zf[:], gd[t][:], COPY, scale=gn_t[:, t : t + 1])
            gained.append(zf)

        for t in range(PACK + 1):
            if t < PACK:
                clip(t)
            if t > 0:
                put_back(t - 1)

        y_w = keep.tile([P, V], I32, name="y_w", align_bytes=64)
        y_s = keep.tile([P, V], U8, name="y_s", align_bytes=64)
        y = [keep.tile([P, PACK, CHUNK], F32, name="y%d" % c, align_bytes=64) for c in range(chunks)]
        out_words = packed_words(out_1)
        woven = [keep.tile([P, CHUNK, PACK], BF16, name="woven%d" % c, align_bytes=64) for c in range(chunks)]
        rounded = [keep.tile([P, CHUNK, PACK], BF16, name="rounded%d" % c, align_bytes=64) for c in range(chunks)]
        z_w = keep.tile([P, V], U32, name="z_w", align_bytes=64)
        z_s = keep.tile([P, V], U8, name="z_s", align_bytes=64)

        def weave(pairs, rows):
            nc.scalar.copy(out=pairs.rearrange("p (c i) t -> p c t i", i=RUN), in_=rows.rearrange("p t (c i) -> p c t i", i=RUN))

        for c in range(chunks):
            if c == 2:
                planes = keep.tile([P, PACK, CHUNK], BF16, name="planes", tag="gd3", align_bytes=64)
            else:
                planes = ring.tile([P, PACK, CHUNK], BF16, name="planes", tag="stage", align_bytes=64)
            entries = look_t[:, c * CHUNK // 16 : (c + 1) * CHUNK // 16]
            for t in range(PACK):
                nc.vector.tensor_copy(out=planes[:, t, :], in_=gained[t][:].indirect(entries))
            for inner in range(0, CHUNK, PIECE):
                weave(woven[c][:, inner : inner + PIECE, :], planes[:, :, inner : inner + PIECE])

        prods = []
        for first in range(0, V, PIECE):
            c, inner = divmod(first, CHUNK)
            cols = slice(first, first + PIECE)
            nc.vector.quantize_mx(
                out=z_w[:, cols].bitcast(FP8X4), scales=z_s[:, cols],
                in_=woven[c][:, inner : inner + PIECE, :].rearrange("p n t -> p (n t)"),
            )
            bank = psum.tile([P, PACK, PIECE], F32, name="prod", tag="bank%d" % (first // PIECE))
            for t in range(PACK):
                nc.tensor.matmul_mx(
                    out=bank[:, t, :], lhsT=w2_dw[:, t, :].bitcast(FP8X4), lhsT_scale=w2_ds[:, t, :],
                    rhs=z_w[:, cols].bitcast(FP8X4), rhs_scale=z_s[:, cols], start=True, stop=True,
                )
            prods.append(bank)

        for first in range(0, V, PIECE):
            c, inner = divmod(first, CHUNK)
            h, place = divmod(first, V // 2)
            part = y[c][:, :, inner : inner + PIECE]
            nc.vector.tensor_tensor(part, prods[first // PIECE][:], res_t[h][:, :, place : place + PIECE], ALU.add)
            weave(rounded[c][:, inner : inner + PIECE, :], part)
            if inner + PIECE == CHUNK:
                nc.sync.dma_start(out=out_rows[:, :, c * CHUNK : (c + 1) * CHUNK], in_=y[c][:])

        for c in range(chunks):
            cols = slice(c * CHUNK, (c + 1) * CHUNK)
            nc.vector.quantize_mx(out=y_w[:, cols].bitcast(FP8X4), scales=y_s[:, cols], in_=rounded[c][:].rearrange("p n t -> p (n t)"))
        for cols in (slice(0, V - CHUNK), slice(V - CHUNK, V)):
            nc.sync.dma_start(out=out_words[:, cols], in_=y_w[:, cols])
        for q in range(QUADS):
            queue = nc.scalar if q % 2 else nc.sync
            queue.dma_start(out=out_2[0, 4 * q : 4 * q + 4, :].bitcast(I32), in_=y_s[32 * q : 32 * q + 4, :].bitcast(I32))
